import numpy as np
import ml_dtypes


def mxq(x, axis, fmt="e4m3"):
    dtype, down = {"e4m3": (ml_dtypes.float8_e4m3fn, 7), "e5m2": (ml_dtypes.float8_e5m2, 14)}[fmt]
    v = np.moveaxis(np.asarray(x, np.float32).astype(ml_dtypes.bfloat16).astype(np.float64), axis, -1)
    blocks = v.reshape(v.shape[:-1] + (-1, 32))
    amax = np.abs(blocks).max(-1, keepdims=True)
    byte = np.maximum(np.where(amax > 0, np.frexp(amax)[1] - 1 + 127, 0) - down, 1)
    scale = np.exp2(byte - 127.0)
    codes = (blocks / scale).astype(np.float32).astype(dtype).astype(np.float64)
    return np.moveaxis((codes * scale).reshape(v.shape), -1, axis)


WIDE = False


def mx_kscale(k):
    if not WIDE:
        return np.ones(k)
    levels = np.array([10, -10, 5, -5, 0])
    if k % 512:
        return np.exp2(np.random.permutation(np.resize(levels, k // 32))).repeat(32)
    a = np.empty((k // 512, 16))
    for p in range(k // 512):
        a[p, :8] = np.random.permutation(np.resize(levels, 8))
        for g in range(8):
            far = levels[np.abs(levels - a[p, g]) >= 10]
            a[p, g + 8] = far[np.random.randint(len(far))]
    return np.exp2(a.ravel()).repeat(32)


def f64(x):
    return np.asarray(x).astype(np.float64)


def striped(idx):
    return np.tile(idx.reshape(-1, 16).T, (8, 1)).astype(np.uint16)


def unstriped(offs):
    return offs[:16].T.reshape(-1).astype(np.int64)


E2M1 = np.array([0.0, 0.5, 1.0, 1.5, 2.0, 3.0, 4.0, 6.0, -0.0, -0.5, -1.0, -1.5, -2.0, -3.0, -4.0, -6.0])


def pack_weight(w, fmt):
    k, n = w.shape
    w = f64(np.asarray(w, np.float32).astype(ml_dtypes.bfloat16)).reshape(k // 32, 32, n)
    amax = np.abs(w).max(1)
    if fmt == "e4m3":
        byte = np.frexp(amax)[1] - 1 + 127 - 7
    else:
        mant, ex = np.frexp(amax / 6.0)
        byte = np.where(mant > 0.5, ex, ex - 1) + 127
    byte = np.clip(np.where(amax > 0, byte, 1), 1, 254)
    scaled = (w * np.exp2(127.0 - byte)[:, None, :]).reshape(k, n).astype(np.float32)
    by_word = np.ascontiguousarray(scaled.reshape(k // 512, 128, 4, n).transpose(0, 1, 3, 2))
    if fmt == "e4m3":
        words = by_word.astype(ml_dtypes.float8_e4m3fn).view(np.uint8)
    else:
        c = by_word.astype(ml_dtypes.float4_e2m1fn).view(np.uint8) & 0xF
        words = (c[..., 0::2] | (c[..., 1::2] << 4)).reshape(k // 512, 128, 2 * n)
    return np.ascontiguousarray(words), np.ascontiguousarray(byte.astype(np.uint8).reshape(k // 512, 16, n))


def unpack_weight(words, scales, fmt):
    g, _, n = scales.shape
    words = np.ascontiguousarray(words).reshape(g, 128, n, -1)
    if fmt == "e4m3":
        vals = words.view(ml_dtypes.float8_e4m3fn).astype(np.float64)
    else:
        nib = np.empty((g, 128, n, 4), np.uint8)
        nib[..., 0::2] = words & 0xF
        nib[..., 1::2] = words >> 4
        vals = E2M1[nib]
    vals = vals * np.repeat(np.exp2(scales.astype(np.float64) - 127.0), 8, axis=1)[..., None]
    return vals.transpose(0, 1, 3, 2).reshape(g * 512, n)


def planes(y):
    n, m = y.shape
    v = y.astype(np.float32).astype(ml_dtypes.bfloat16).astype(np.float64).reshape(n // 32, 32, m)
    top = np.abs(v).max(1)
    byte = np.clip(np.where(top > 0, np.frexp(top)[1] - 1 + 127 - 7, 1), 1, 254)
    codes = (v * np.exp2(127.0 - byte)[:, None, :]).reshape(n, m).astype(np.float32).astype(ml_dtypes.float8_e4m3fn).view(np.uint8)
    words = codes.reshape(n // 512, 128, 4, m).transpose(0, 1, 3, 2)
    return np.ascontiguousarray(words), np.ascontiguousarray(byte.astype(np.uint8).reshape(n // 512, 16, m))


def relu(v):
    return np.maximum(v, 0.0)


K, T, E, C, F, D, H = 1024, 512, 4, 128, 2, 256, 512
N = 512


def by_expert(wq, xq, E, C):
    return np.concatenate([wq[e].T @ xq[:, e * C:(e + 1) * C] for e in range(E)], axis=1)


def setup_inputs():
    n = np.random.standard_normal
    s = mx_kscale(K)
    u = mx_kscale(H)
    slot_token = np.random.permutation(T)[:E * C]
    slots2 = np.random.permutation(T)[:F * D]
    x = pack_weight(n((K, T)) * s[:, None], "e4m3")
    w = [pack_weight(m, "e2m1") for m in n((E, K, N)) / np.sqrt(K) / s[None, :, None]]
    wa = [pack_weight(m, "e4m3") for m in n((F, K, H)) / np.sqrt(K) / s[None, :, None] * u]
    wb = [pack_weight(m, "e4m3") for m in n((F, H, N)) / np.sqrt(H) / u[None, :, None]]
    return {
        "x_words": x[0],
        "x_scales": x[1],
        "w_words": np.stack([m[0] for m in w]),
        "w_scales": np.stack([m[1] for m in w]),
        "wa_words": np.stack([m[0] for m in wa]),
        "wa_scales": np.stack([m[1] for m in wa]),
        "wb_words": np.stack([m[0] for m in wb]),
        "wb_scales": np.stack([m[1] for m in wb]),
        "gate": np.tile(np.random.uniform(0.2, 1.0, E * C), (128, 1)).astype(np.float32),
        "gate2": (np.tile(np.random.uniform(0.2, 1.0, F * D), (128, 1))).astype(np.float32),
        "offs": striped(slot_token),
        "offs2": striped(slots2),
    }


def reference(x_words, x_scales, w_words, w_scales, wa_words, wa_scales, wb_words, wb_scales, gate, gate2, offs, offs2):
    w = np.stack([unpack_weight(w_words[e], w_scales[e], "e2m1") for e in range(E)])
    wa = np.stack([unpack_weight(wa_words[e], wa_scales[e], "e4m3") for e in range(F)])
    wb = np.stack([unpack_weight(wb_words[e], wb_scales[e], "e4m3") for e in range(F)])
    idx, idx2 = unstriped(offs), unstriped(offs2)
    x = unpack_weight(x_words, x_scales, "e4m3")
    y = by_expert(w, x[:, idx], E, C)
    h = relu(by_expert(wa, x[:, idx2], F, D))
    z = by_expert(wb, mxq(h, 0, "e4m3"), F, D)
    out = np.zeros((N, T))
    out[:, idx] = f64(gate[:1]) * y
    out[:, idx2] += f64(gate2[:1]) * z
    out_0 = out
    return (out_0,) + planes(out_0)

@@ -1,0 +1,240 @@
+from contextlib import ExitStack
+
+import concourse.mybir as mybir
+from concourse.masks import make_identity
+
+K, T, E, C, F, D, H, N = 1024, 512, 4, 128, 2, 256, 512, 512
+FLOPS = 2 * T * (K * N + K * H + H * N)
+
+F32 = mybir.dt.float32
+BF16 = mybir.dt.bfloat16
+I32 = mybir.dt.int32
+U32 = mybir.dt.uint32
+U16 = mybir.dt.uint16
+U8 = mybir.dt.uint8
+FP8X4 = mybir.dt.float8_e4m3fn_x4
+FP4X4 = mybir.dt.float4_e2m1fn_x4
+COPY = mybir.ActivationFunctionType.Copy
+RELU = mybir.ActivationFunctionType.Relu
+ADD = mybir.AluOpType.add
+
+P = 128
+PACK = 4
+PASSES = K // (P * PACK)
+QUADS = 4
+TILES = T // P
+WIDE = 704
+SHIFT_ROWS = 112
+HALF = T // 2
+
+
+def tile_moe_mlr_relu_kernel(
+    tc, x_words, x_scales, w_words, w_scales, wa_words, wa_scales, wb_words, wb_scales,
+    gate, gate2, offs, offs2, out_0, out_1, out_2,
+):
+    nc = tc.nc
+    with ExitStack() as ctx:
+        sb = ctx.enter_context(tc.tile_pool(name="sb", bufs=1))
+        ps = ctx.enter_context(tc.psum_pool(name="ps", bufs=1))
+
+        def tile(shape, dtype, name):
+            return sb.tile(shape, dtype, name=name, align_bytes=64)
+
+        def bank(b, shape, name):
+            return ps.tile(shape, F32, name=name, tag="bank%d" % b)
+
+        def entries(lst, first, count):
+            return lst[:, first // 16:(first + count) // 16]
+
+        def zeroed(engine, shape, name):
+            t = tile(shape, U8, name)
+            engine.memset(t[:].bitcast(I32), 0)
+            return t
+
+        xs = zeroed(nc.vector, [P, WIDE], "xs")
+        ws = zeroed(nc.vector, [P, E * PASSES * N], "ws")
+        gs_low = zeroed(nc.vector, [P, T], "gs_low")
+        ident = tile([P, P], F32, "ident")
+        make_identity(nc, ident[:])
+        gate_rows = tile([P, P], F32, "gate_rows")
+        nc.gpsimd.memset(gate_rows[:], 0.0)
+        gate2_rows = tile([P, P], F32, "gate2_rows")
+        nc.gpsimd.memset(gate2_rows[:], 0.0)
+        was = zeroed(nc.gpsimd, [P, H], "was")
+        wbs = zeroed(nc.gpsimd, [P, N], "wbs")
+
+        lst = sb.tile([P, T // 16], U16, name="lst")
+        nc.sync.dma_start(lst[:], offs)
+        for q in range(QUADS):
+            nc.sync.dma_start(xs[32 * q:32 * q + 4 * PASSES, 0:T].bitcast(I32), x_scales[:, 4 * q:4 * q + 4, :].bitcast(I32))
+        xw = tile([P, PASSES, T], I32, "xw")
+        nc.sync.dma_start(xw[:], x_words.rearrange("s p t d -> p s (t d)").bitcast(I32))
+        nc.sync.dma_start(gate_rows[0:TILES, :], gate[0:1, :].rearrange("a (j m) -> (a j) m", m=P))
+        lst2 = sb.tile([P, T // 16], U16, name="lst2")
+        nc.sync.dma_start(lst2[:], offs2)
+        for q in range(QUADS):
+            nc.sync.dma_start(
+                ws[32 * q:32 * q + 4, :].bitcast(I32).rearrange("r (g n) -> r g n", g=E * PASSES),
+                w_scales[:, :, 4 * q:4 * q + 4, :].rearrange("e s r n -> r (e s) n").bitcast(I32))
+        ww = []
+        for e in range(E):
+            t = tile([P, PASSES, 2 * N], U8, "ww%d" % e)
+            nc.sync.dma_start(t[:].bitcast(I32), w_words[e].rearrange("s p b -> p s b").bitcast(I32))
+            ww.append(t)
+        nc.sync.dma_start(gate2_rows[0:TILES, :], gate2[0:1, :].rearrange("a (j m) -> (a j) m", m=P))
+        for q in range(QUADS):
+            nc.sync.dma_start(was[32 * q:32 * q + 4 * F * PASSES, :].bitcast(I32),
+                              wa_scales[:, :, 4 * q:4 * q + 4, :].rearrange("f s r n -> (f s) r n").bitcast(I32))
+        waw = []
+        for f in range(F):
+            t = tile([P, PASSES, H], I32, "waw%d" % f)
+            nc.sync.dma_start(t[:], wa_words[f].rearrange("s p i d -> p s (i d)").bitcast(I32))
+            waw.append(t)
+        for q in range(QUADS):
+            nc.sync.dma_start(wbs[32 * q:32 * q + 4 * F, :].bitcast(I32),
+                              wb_scales[:, :, 4 * q:4 * q + 4, :].rearrange("f s r n -> (f s) r n").bitcast(I32))
+        wbw = tile([P, F, N], I32, "wbw")
+        nc.sync.dma_start(wbw[:], wb_words.rearrange("f s p n d -> p (f s) (n d)").bitcast(I32))
+
+        def gather_tokens(offsets, name):
+            scales = tile([P, T], U8, name + "_scales")
+            nc.vector.tensor_copy(scales[:], xs[:].indirect(offsets[:]))
+            words = {}
+            for h in range(2):
+                for s in range(PASSES):
+                    words[h, s] = tile([P, HALF], U32, "%s_words%d%d" % (name, h, s))
+                    nc.vector.tensor_copy(words[h, s][:], xw[:, s, :].bitcast(U32).indirect(entries(offsets, h * HALF, HALF)))
+            return scales, words
+
+        gs, gw = gather_tokens(lst, "g")
+        nc.scalar.dma_start(gs_low[0:SHIFT_ROWS, :].bitcast(I32), gs[4:4 + SHIFT_ROWS, :].bitcast(I32))
+        gs2, gw2 = gather_tokens(lst2, "g2")
+
+        def token_words(words, j, s):
+            return words[j // 2, s][:, (j % 2) * P:(j % 2 + 1) * P].bitcast(FP8X4)
+
+        def gate_columns(rows, b, name):
+            turned = bank(b, [P, P], name + "_turned")
+            nc.tensor.transpose(turned[:], rows[:], ident[:])
+            cols = tile([P, TILES], F32, name)
+            nc.scalar.activation(cols[:], turned[:, 0:TILES], COPY)
+            return cols
+
+        g_cols = gate_columns(gate_rows, 6, "g_cols")
+
+        def gated_rows(acc, cols, j, name):
+            rows = tile([P, PACK, P], F32, name)
+            nc.scalar.activation(rows[:], acc[:].rearrange("s (m d) -> s d m", d=PACK), COPY, scale=cols[:, j:j + 1])
+            return rows
+
+        y_front = tile([P, 2, T], F32, "y_front")
+        y_rows = []
+        for e in range(E):
+            acc = bank(e, [P, N], "y_acc%d" % e)
+            for s in range(PASSES):
+                plane = (gs, gs_low)[s]
+                g = e * PASSES + s
+                nc.tensor.matmul_mx(acc[:], lhsT=token_words(gw, e, s), lhsT_scale=plane[:, e * P:(e + 1) * P],
+                                    rhs=ww[e][:, s, :].bitcast(FP4X4), rhs_scale=ws[:, g * N:(g + 1) * N],
+                                    start=s == 0, stop=s == PASSES - 1)
+            y_rows.append(gated_rows(acc, g_cols, e, "y_rows%d" % e))
+            turned = bank(4 + e % 2, [P, 2, P], "y_turned%d" % e)
+            for d in range(2):
+                nc.tensor.transpose(turned[:, d, :], y_rows[e][:, d, :], ident[:])
+            nc.scalar.copy(y_front[:, :, e * P:(e + 1) * P], turned[:])
+
+        o_win = [tile([P, T if d < 2 else WIDE], F32, "o_win%d" % d) for d in range(PACK)]
+        for first, count in ((0, P), (P, P), (2 * P, 2 * P)):
+            for d in range(2):
+                nc.vector.tensor_copy(o_win[d][:].indirect(entries(lst, first, count)), y_front[:, d, first:first + count])
+
+        g2_cols = gate_columns(gate2_rows, 6, "g2_cols")
+
+        hq, hs = [], []
+        for f in range(F):
+            h_turned = bank(6 + f, [P, 2, 2, P], "h_turned%d" % f)
+            for jj in range(2):
+                j = 2 * f + jj
+                acc = bank(j, [P, H], "h_acc%d" % j)
+                for s in range(PASSES):
+                    nc.tensor.matmul_mx(acc[:], lhsT=token_words(gw2, j, s), lhsT_scale=gs2[4 * s:P, j * P:(j + 1) * P],
+                                        rhs=waw[f][:, s, :].bitcast(FP8X4), rhs_scale=was[4 * (f * PASSES + s):P, :],
+                                        start=s == 0, stop=s == PASSES - 1)
+                h_rows = tile([P, 2, P, 2], BF16, "h_rows%d" % j)
+                nc.scalar.activation(h_rows[:], acc[:].rearrange("s (p u e) -> s u p e", u=2, e=2), RELU)
+                pairs = h_rows[:].rearrange("s u p e -> s (u p e)").bitcast(F32)
+                for u in range(2):
+                    nc.tensor.transpose(h_turned[:, jj, u, :], pairs[:, u * P:(u + 1) * P], ident[:])
+            hb = tile([P, 2, P, 2], F32, "hb%d" % f)
+            nc.scalar.copy(hb[:], h_turned[:].rearrange("p j u s -> p j s u"))
+            hq.append(tile([P, D], U32, "hq%d" % f))
+            hs.append(tile([P, D], U8, "hs%d" % f))
+            nc.vector.quantize_mx(hq[f][:].bitcast(FP8X4), hs[f][:], hb[:].rearrange("p j s u -> p (j s u)").bitcast(BF16))
+
+        def slot_columns(rows, d, b, name):
+            turned = bank(b, [P, T], name + "_turned")
+            for j in range(TILES):
+                nc.tensor.transpose(turned[:, j * P:(j + 1) * P], rows[j][:, d, :], ident[:])
+            cols = tile([P, T], F32, name)
+            nc.scalar.copy(cols[:], turned[:])
+            return cols
+
+        for d in range(2, PACK):
+            cols = slot_columns(y_rows, d, 7, "y_cols%d" % d)
+            nc.vector.tensor_copy(o_win[d][:].indirect(lst[:]), cols[:])
+
+        z_rows = []
+        for j in range(TILES):
+            f, jj = divmod(j, 2)
+            acc = bank(j, [P, N], "z_acc%d" % j)
+            nc.tensor.matmul_mx(acc[:], lhsT=hq[f][:, jj * P:(jj + 1) * P].bitcast(FP8X4), lhsT_scale=hs[f][:, jj * P:(jj + 1) * P],
+                                rhs=wbw[:, f, :].bitcast(FP8X4), rhs_scale=wbs[4 * f:P, :], start=True, stop=True)
+            z_rows.append(gated_rows(acc, g2_cols, j, "z_rows%d" % j))
+
+        total = tile([P, PACK, T], F32, "total")
+        out_rows = out_0.rearrange("(p d) t -> p d t", d=PACK)
+        z_win = []
+        for d in range(PACK):
+            cols = slot_columns(z_rows, d, 4 + d % 2, "z_cols%d" % d)
+            z_win.append(tile([P, WIDE], F32, "z_win%d" % d))
+            nc.vector.tensor_copy(z_win[d][:].indirect(lst2[:]), cols[:])
+
+        for d in range(PACK - 1):
+            summed = bank(2 * (d % 2), [P, T], "summed%d" % d)
+            for j in range(TILES):
+                for i, win in enumerate((o_win[d], z_win[d])):
+                    nc.tensor.matmul(summed[:, j * P:(j + 1) * P], lhsT=win[:, j * P:(j + 1) * P], rhs=ident[:],
+                                     is_transpose=True, start=i == 0, stop=i == 1)
+            by_token = tile([P, T], F32, "by_token%d" % d)
+            nc.scalar.copy(by_token[:], summed[:])
+            back = bank(2 * (d % 2) + 1, [P, T], "back%d" % d)
+            for j in range(TILES):
+                nc.tensor.transpose(back[:, j * P:(j + 1) * P], by_token[:, j * P:(j + 1) * P], ident[:])
+            nc.scalar.copy(total[:, d, :], back[:])
+            nc.sync.dma_start(out_rows[:, d, :], total[:, d, :])
+
+        last = PACK - 1
+        for h in (1, 0):
+            cols = slice(h * HALF, (h + 1) * HALF)
+            nc.vector.tensor_tensor(total[:, last, cols], o_win[last][:, cols], z_win[last][:, cols], ADD)
+        nc.sync.dma_start(out_rows[:, last, :], total[:, last, :])
+
+        grouped = tile([P, T, PACK], BF16, "grouped")
+
+        def regroup(engine_copy, first, count):
+            engine_copy(grouped[:, first:first + count, :].rearrange("p (c i) d -> p c d i", i=4),
+                        total[:, :, first:first + count].rearrange("p d (c i) -> p c d i", i=4))
+
+        regroup(nc.scalar.copy, 3 * P, P)
+        regroup(nc.vector.tensor_copy, 2 * P, P)
+        regroup(nc.vector.tensor_copy, 0, HALF)
+        out_scales = tile([P, T], U8, "out_scales")
+        words_out = out_1.rearrange("s p t d -> p (s t d)").bitcast(I32)
+        for h in (1, 0):
+            cols = slice(h * HALF, (h + 1) * HALF)
+            codes = tile([P, HALF], U32, "codes%d" % h)
+            nc.vector.quantize_mx(codes[:].bitcast(FP8X4), out_scales[:, cols], grouped[:, cols, :].rearrange("p t d -> p (t d)"))
+            nc.sync.dma_start(words_out[:, cols], codes[:].bitcast(I32))
+        for q in range(QUADS):
+            queue = (nc.scalar, nc.sync)[q % 2]
+            queue.dma_start(out_2[0, 4 * q:4 * q + 4, :].bitcast(I32), out_scales[32 * q:32 * q + 4, :].bitcast(I32))

@@ -24,7 +24,7 @@ PASSES = K // (P * PACK)
 QUADS = 4
 TILES = T // P
 WIDE = 704
-SHIFT_ROWS = 112
+SHIFT_ROWS = 100
 HALF = T // 2
 
 
@@ -37,8 +37,8 @@ def tile_moe_mlr_relu_kernel(
         sb = ctx.enter_context(tc.tile_pool(name="sb", bufs=1))
         ps = ctx.enter_context(tc.psum_pool(name="ps", bufs=1))
 
-        def tile(shape, dtype, name):
-            return sb.tile(shape, dtype, name=name, align_bytes=64)
+        def tile(shape, dtype, name, tag=None):
+            return sb.tile(shape, dtype, name=name, tag=tag or name, align_bytes=64)
 
         def bank(b, shape, name):
             return ps.tile(shape, F32, name=name, tag="bank%d" % b)
@@ -46,111 +46,110 @@ def tile_moe_mlr_relu_kernel(
         def entries(lst, first, count):
             return lst[:, first // 16:(first + count) // 16]
 
-        def zeroed(engine, shape, name):
-            t = tile(shape, U8, name)
+        def zeroed(engine, shape, name, tag=None):
+            t = tile(shape, U8, name, tag)
             engine.memset(t[:].bitcast(I32), 0)
             return t
 
-        xs = zeroed(nc.vector, [P, WIDE], "xs")
+        xs = zeroed(nc.gpsimd, [P, WIDE], "xs")
         ws = zeroed(nc.vector, [P, E * PASSES * N], "ws")
         gs_low = zeroed(nc.vector, [P, T], "gs_low")
-        ident = tile([P, P], F32, "ident")
-        make_identity(nc, ident[:])
         gate_rows = tile([P, P], F32, "gate_rows")
         nc.gpsimd.memset(gate_rows[:], 0.0)
-        gate2_rows = tile([P, P], F32, "gate2_rows")
-        nc.gpsimd.memset(gate2_rows[:], 0.0)
-        was = zeroed(nc.gpsimd, [P, H], "was")
-        wbs = zeroed(nc.gpsimd, [P, N], "wbs")
+        ident = tile([P, P], F32, "ident")
+        make_identity(nc, ident[:])
+        adapter_scales = zeroed(nc.gpsimd, [P, H + N], "adapter_scales")
+        was, wbs = adapter_scales[:, 0:H], adapter_scales[:, H:H + N]
+
+        def load_expert_pair(h):
+            words = tile([P, 2 * PASSES, 2 * N], U8, "ww%d" % h)
+            nc.sync.dma_start(words[:].bitcast(I32), w_words[2 * h:2 * h + 2].rearrange("e s p b -> p (e s) b").bitcast(I32))
+            return words
+
+        def load_stacked_scales(plane, rows):
+            for q in range(QUADS):
+                nc.sync.dma_start(plane[32 * q:32 * q + 4 * rows.shape[0], :].bitcast(I32), rows[:, 4 * q:4 * q + 4, :].bitcast(I32))
 
         lst = sb.tile([P, T // 16], U16, name="lst")
         nc.sync.dma_start(lst[:], offs)
-        for q in range(QUADS):
-            nc.sync.dma_start(xs[32 * q:32 * q + 4 * PASSES, 0:T].bitcast(I32), x_scales[:, 4 * q:4 * q + 4, :].bitcast(I32))
+        load_stacked_scales(xs[:, 0:T], x_scales)
         xw = tile([P, PASSES, T], I32, "xw")
         nc.sync.dma_start(xw[:], x_words.rearrange("s p t d -> p s (t d)").bitcast(I32))
-        nc.sync.dma_start(gate_rows[0:TILES, :], gate[0:1, :].rearrange("a (j m) -> (a j) m", m=P))
         lst2 = sb.tile([P, T // 16], U16, name="lst2")
         nc.sync.dma_start(lst2[:], offs2)
+        ww = [load_expert_pair(0)]
         for q in range(QUADS):
             nc.sync.dma_start(
                 ws[32 * q:32 * q + 4, :].bitcast(I32).rearrange("r (g n) -> r g n", g=E * PASSES),
                 w_scales[:, :, 4 * q:4 * q + 4, :].rearrange("e s r n -> r (e s) n").bitcast(I32))
-        ww = []
-        for e in range(E):
-            t = tile([P, PASSES, 2 * N], U8, "ww%d" % e)
-            nc.sync.dma_start(t[:].bitcast(I32), w_words[e].rearrange("s p b -> p s b").bitcast(I32))
-            ww.append(t)
-        nc.sync.dma_start(gate2_rows[0:TILES, :], gate2[0:1, :].rearrange("a (j m) -> (a j) m", m=P))
-        for q in range(QUADS):
-            nc.sync.dma_start(was[32 * q:32 * q + 4 * F * PASSES, :].bitcast(I32),
-                              wa_scales[:, :, 4 * q:4 * q + 4, :].rearrange("f s r n -> (f s) r n").bitcast(I32))
-        waw = []
-        for f in range(F):
-            t = tile([P, PASSES, H], I32, "waw%d" % f)
-            nc.sync.dma_start(t[:], wa_words[f].rearrange("s p i d -> p s (i d)").bitcast(I32))
-            waw.append(t)
-        for q in range(QUADS):
-            nc.sync.dma_start(wbs[32 * q:32 * q + 4 * F, :].bitcast(I32),
-                              wb_scales[:, :, 4 * q:4 * q + 4, :].rearrange("f s r n -> (f s) r n").bitcast(I32))
+        for i, row in enumerate((gate, gate2)):
+            nc.sync.dma_start(gate_rows[i * TILES:(i + 1) * TILES, :], row[0:1, :].rearrange("a (j m) -> (a j) m", m=P))
+        ww.append(load_expert_pair(1))
+        load_stacked_scales(was, wa_scales.rearrange("f s b n -> (f s) b n"))
+        waw = tile([P, F * PASSES, H], I32, "waw")
+        nc.sync.dma_start(waw[:], wa_words.rearrange("f s p i d -> p (f s) (i d)").bitcast(I32))
+        load_stacked_scales(wbs, wb_scales.rearrange("f s b n -> (f s) b n"))
         wbw = tile([P, F, N], I32, "wbw")
         nc.sync.dma_start(wbw[:], wb_words.rearrange("f s p n d -> p (f s) (n d)").bitcast(I32))
 
-        def gather_tokens(offsets, name):
-            scales = tile([P, T], U8, name + "_scales")
+        def gather_scales(offsets, name):
+            scales = tile([P, T], U8, name)
             nc.vector.tensor_copy(scales[:], xs[:].indirect(offsets[:]))
-            words = {}
-            for h in range(2):
-                for s in range(PASSES):
-                    words[h, s] = tile([P, HALF], U32, "%s_words%d%d" % (name, h, s))
-                    nc.vector.tensor_copy(words[h, s][:], xw[:, s, :].bitcast(U32).indirect(entries(offsets, h * HALF, HALF)))
-            return scales, words
+            return scales
 
-        gs, gw = gather_tokens(lst, "g")
+        def gather_words(offsets, h, name):
+            words = []
+            for s in range(PASSES):
+                words.append(tile([P, HALF], U32, "%s%d%d" % (name, h, s)))
+                nc.vector.tensor_copy(words[s][:], xw[:, s, :].bitcast(U32).indirect(entries(offsets, h * HALF, HALF)))
+            return words
+
+        gs = gather_scales(lst, "gs")
         nc.scalar.dma_start(gs_low[0:SHIFT_ROWS, :].bitcast(I32), gs[4:4 + SHIFT_ROWS, :].bitcast(I32))
-        gs2, gw2 = gather_tokens(lst2, "g2")
+        gw = [gather_words(lst, 0, "gw")]
+        gs2 = gather_scales(lst2, "gs2")
+        gw.append(gather_words(lst, 1, "gw"))
+        gw2 = [gather_words(lst2, h, "gw2") for h in range(2)]
+
 
         def token_words(words, j, s):
-            return words[j // 2, s][:, (j % 2) * P:(j % 2 + 1) * P].bitcast(FP8X4)
+            return words[j // 2][s][:, (j % 2) * P:(j % 2 + 1) * P].bitcast(FP8X4)
 
-        def gate_columns(rows, b, name):
-            turned = bank(b, [P, P], name + "_turned")
-            nc.tensor.transpose(turned[:], rows[:], ident[:])
-            cols = tile([P, TILES], F32, name)
-            nc.scalar.activation(cols[:], turned[:, 0:TILES], COPY)
-            return cols
+        gates_turned = bank(6, [P, P], "gates_turned")
+        nc.tensor.transpose(gates_turned[:], gate_rows[:], ident[:])
+        gate_cols = tile([P, 2 * TILES], F32, "gate_cols")
+        nc.scalar.activation(gate_cols[:], gates_turned[:, 0:2 * TILES], COPY)
 
-        g_cols = gate_columns(gate_rows, 6, "g_cols")
-
-        def gated_rows(acc, cols, j, name):
-            rows = tile([P, PACK, P], F32, name)
-            nc.scalar.activation(rows[:], acc[:].rearrange("s (m d) -> s d m", d=PACK), COPY, scale=cols[:, j:j + 1])
+        def gated_rows(acc, col, first, count, name):
+            rows = tile([P, count, P], F32, name)
+            nc.scalar.activation(rows[:], acc[:].rearrange("s (m d) -> s d m", d=PACK)[:, first:first + count, :], COPY,
+                                 scale=gate_cols[:, col:col + 1])
             return rows
 
         y_front = tile([P, 2, T], F32, "y_front")
-        y_rows = []
-        for e in range(E):
-            acc = bank(e, [P, N], "y_acc%d" % e)
+        y_acc = [bank(e, [P, N], "y_acc%d" % e) for e in range(E)]
+        for h in range(2):
             for s in range(PASSES):
-                plane = (gs, gs_low)[s]
-                g = e * PASSES + s
-                nc.tensor.matmul_mx(acc[:], lhsT=token_words(gw, e, s), lhsT_scale=plane[:, e * P:(e + 1) * P],
-                                    rhs=ww[e][:, s, :].bitcast(FP4X4), rhs_scale=ws[:, g * N:(g + 1) * N],
-                                    start=s == 0, stop=s == PASSES - 1)
-            y_rows.append(gated_rows(acc, g_cols, e, "y_rows%d" % e))
-            turned = bank(4 + e % 2, [P, 2, P], "y_turned%d" % e)
-            for d in range(2):
-                nc.tensor.transpose(turned[:, d, :], y_rows[e][:, d, :], ident[:])
-            nc.scalar.copy(y_front[:, :, e * P:(e + 1) * P], turned[:])
+                for e in (2 * h, 2 * h + 1):
+                    g = e * PASSES + s
+                    nc.tensor.matmul_mx(y_acc[e][:], lhsT=token_words(gw, e, s), lhsT_scale=(gs, gs_low)[s][:, e * P:(e + 1) * P],
+                                        rhs=ww[h][:, g % (2 * PASSES), :].bitcast(FP4X4), rhs_scale=ws[:, g * N:(g + 1) * N],
+                                        start=s == 0, stop=s == PASSES - 1)
+            for e in (2 * h, 2 * h + 1):
+                rows = gated_rows(y_acc[e], e, 0, 2, "y_rows_front%d" % e)
+                turned = bank(4 + e % 2, [P, 2, P], "y_turned%d" % e)
+                for d in range(2):
+                    nc.tensor.transpose(turned[:, d, :], rows[:, d, :], ident[:])
+                nc.scalar.copy(y_front[:, :, e * P:(e + 1) * P], turned[:])
 
         o_win = [tile([P, T if d < 2 else WIDE], F32, "o_win%d" % d) for d in range(PACK)]
         for first, count in ((0, P), (P, P), (2 * P, 2 * P)):
             for d in range(2):
                 nc.vector.tensor_copy(o_win[d][:].indirect(entries(lst, first, count)), y_front[:, d, first:first + count])
 
-        g2_cols = gate_columns(gate2_rows, 6, "g2_cols")
+        y_rows = [gated_rows(y_acc[e], e, 2, 2, "y_rows_back%d" % e) for e in range(E)]
 
-        hq, hs = [], []
+        hb = tile([P, TILES, P, 2], F32, "hb")
         for f in range(F):
             h_turned = bank(6 + f, [P, 2, 2, P], "h_turned%d" % f)
             for jj in range(2):
@@ -158,18 +157,17 @@ def tile_moe_mlr_relu_kernel(
                 acc = bank(j, [P, H], "h_acc%d" % j)
                 for s in range(PASSES):
                     nc.tensor.matmul_mx(acc[:], lhsT=token_words(gw2, j, s), lhsT_scale=gs2[4 * s:P, j * P:(j + 1) * P],
-                                        rhs=waw[f][:, s, :].bitcast(FP8X4), rhs_scale=was[4 * (f * PASSES + s):P, :],
+                                        rhs=waw[:, f * PASSES + s, :].bitcast(FP8X4), rhs_scale=was[4 * (f * PASSES + s):P, :],
                                         start=s == 0, stop=s == PASSES - 1)
                 h_rows = tile([P, 2, P, 2], BF16, "h_rows%d" % j)
                 nc.scalar.activation(h_rows[:], acc[:].rearrange("s (p u e) -> s u p e", u=2, e=2), RELU)
                 pairs = h_rows[:].rearrange("s u p e -> s (u p e)").bitcast(F32)
                 for u in range(2):
                     nc.tensor.transpose(h_turned[:, jj, u, :], pairs[:, u * P:(u + 1) * P], ident[:])
-            hb = tile([P, 2, P, 2], F32, "hb%d" % f)
-            nc.scalar.copy(hb[:], h_turned[:].rearrange("p j u s -> p j s u"))
-            hq.append(tile([P, D], U32, "hq%d" % f))
-            hs.append(tile([P, D], U8, "hs%d" % f))
-            nc.vector.quantize_mx(hq[f][:].bitcast(FP8X4), hs[f][:], hb[:].rearrange("p j s u -> p (j s u)").bitcast(BF16))
+            nc.scalar.copy(hb[:, 2 * f:2 * f + 2, :, :], h_turned[:].rearrange("p j u s -> p j s u"))
+        hq = tile([P, T], U32, "hq")
+        hs = tile([P, T], U8, "hs")
+        nc.vector.quantize_mx(hq[:].bitcast(FP8X4), hs[:], hb[:].rearrange("p j s u -> p (j s u)").bitcast(BF16))
 
         def slot_columns(rows, d, b, name):
             turned = bank(b, [P, T], name + "_turned")
@@ -180,37 +178,41 @@ def tile_moe_mlr_relu_kernel(
             return cols
 
         for d in range(2, PACK):
-            cols = slot_columns(y_rows, d, 7, "y_cols%d" % d)
+            cols = slot_columns(y_rows, d - 2, 7, "y_cols%d" % d)
             nc.vector.tensor_copy(o_win[d][:].indirect(lst[:]), cols[:])
 
         z_rows = []
         for j in range(TILES):
-            f, jj = divmod(j, 2)
+            f = j // 2
             acc = bank(j, [P, N], "z_acc%d" % j)
-            nc.tensor.matmul_mx(acc[:], lhsT=hq[f][:, jj * P:(jj + 1) * P].bitcast(FP8X4), lhsT_scale=hs[f][:, jj * P:(jj + 1) * P],
+            nc.tensor.matmul_mx(acc[:], lhsT=hq[:, j * P:(j + 1) * P].bitcast(FP8X4), lhsT_scale=hs[:, j * P:(j + 1) * P],
                                 rhs=wbw[:, f, :].bitcast(FP8X4), rhs_scale=wbs[4 * f:P, :], start=True, stop=True)
-            z_rows.append(gated_rows(acc, g2_cols, j, "z_rows%d" % j))
+            z_rows.append(gated_rows(acc, TILES + j, 0, PACK, "z_rows%d" % j))
 
         total = tile([P, PACK, T], F32, "total")
         out_rows = out_0.rearrange("(p d) t -> p d t", d=PACK)
         z_win = []
         for d in range(PACK):
-            cols = slot_columns(z_rows, d, 4 + d % 2, "z_cols%d" % d)
+            cols = slot_columns(z_rows, d, 4 + d, "z_cols%d" % d)
             z_win.append(tile([P, WIDE], F32, "z_win%d" % d))
             nc.vector.tensor_copy(z_win[d][:].indirect(lst2[:]), cols[:])
 
         for d in range(PACK - 1):
-            summed = bank(2 * (d % 2), [P, T], "summed%d" % d)
-            for j in range(TILES):
-                for i, win in enumerate((o_win[d], z_win[d])):
-                    nc.tensor.matmul(summed[:, j * P:(j + 1) * P], lhsT=win[:, j * P:(j + 1) * P], rhs=ident[:],
-                                     is_transpose=True, start=i == 0, stop=i == 1)
-            by_token = tile([P, T], F32, "by_token%d" % d)
-            nc.scalar.copy(by_token[:], summed[:])
-            back = bank(2 * (d % 2) + 1, [P, T], "back%d" % d)
-            for j in range(TILES):
-                nc.tensor.transpose(back[:, j * P:(j + 1) * P], by_token[:, j * P:(j + 1) * P], ident[:])
-            nc.scalar.copy(total[:, d, :], back[:])
+            by_token = []
+            for h in range(2):
+                summed = bank(h, [P, HALF], "summed%d%d" % (d, h))
+                for jj in range(2):
+                    j = 2 * h + jj
+                    for i, win in enumerate((o_win[d], z_win[d])):
+                        nc.tensor.matmul(summed[:, jj * P:(jj + 1) * P], lhsT=win[:, j * P:(j + 1) * P], rhs=ident[:],
+                                         is_transpose=True, start=i == 0, stop=i == 1)
+                by_token.append(tile([P, HALF], F32, "by_token%d%d" % (d, h)))
+                nc.scalar.copy(by_token[h][:], summed[:])
+            for h in range(2):
+                back = bank(2 + h, [P, HALF], "back%d%d" % (d, h))
+                for jj in range(2):
+                    nc.tensor.transpose(back[:, jj * P:(jj + 1) * P], by_token[h][:, jj * P:(jj + 1) * P], ident[:])
+                nc.scalar.copy(total[:, d, h * HALF:(h + 1) * HALF], back[:])
             nc.sync.dma_start(out_rows[:, d, :], total[:, d, :])
 
         last = PACK - 1

@@ -224,8 +224,8 @@ def tile_moe_mlr_relu_kernel(
         grouped = tile([P, T, PACK], BF16, "grouped")
 
         def regroup(engine_copy, first, count):
-            engine_copy(grouped[:, first:first + count, :].rearrange("p (c i) d -> p c d i", i=4),
-                        total[:, :, first:first + count].rearrange("p d (c i) -> p c d i", i=4))
+            engine_copy(grouped[:, first:first + count, :].rearrange("p (c i) d -> p c d i", i=2),
+                        total[:, :, first:first + count].rearrange("p d (c i) -> p c d i", i=2))
 
         regroup(nc.scalar.copy, 3 * P, P)
         regroup(nc.vector.tensor_copy, 2 * P, P)

from contextlib import ExitStack

import concourse.mybir as mybir
from concourse.masks import make_identity

K, T, E, C, F, D, H, N = 1024, 512, 4, 128, 2, 256, 512, 512
FLOPS = 2 * T * (K * N + K * H + H * N)

F32 = mybir.dt.float32
BF16 = mybir.dt.bfloat16
I32 = mybir.dt.int32
U32 = mybir.dt.uint32
U16 = mybir.dt.uint16
U8 = mybir.dt.uint8
FP8X4 = mybir.dt.float8_e4m3fn_x4
FP4X4 = mybir.dt.float4_e2m1fn_x4
COPY = mybir.ActivationFunctionType.Copy
RELU = mybir.ActivationFunctionType.Relu
ADD = mybir.AluOpType.add

P = 128
PACK = 4
PASSES = K // (P * PACK)
QUADS = 4
TILES = T // P
WIDE = 704
SHIFT_ROWS = 100
HALF = T // 2


def tile_moe_mlr_relu_kernel(
    tc, x_words, x_scales, w_words, w_scales, wa_words, wa_scales, wb_words, wb_scales,
    gate, gate2, offs, offs2, out_0, out_1, out_2,
):
    nc = tc.nc
    with ExitStack() as ctx:
        sb = ctx.enter_context(tc.tile_pool(name="sb", bufs=1))
        ps = ctx.enter_context(tc.psum_pool(name="ps", bufs=1))

        def tile(shape, dtype, name, tag=None):
            return sb.tile(shape, dtype, name=name, tag=tag or name, align_bytes=64)

        def bank(b, shape, name):
            return ps.tile(shape, F32, name=name, tag="bank%d" % b)

        def entries(lst, first, count):
            return lst[:, first // 16:(first + count) // 16]

        def zeroed(engine, shape, name, tag=None):
            t = tile(shape, U8, name, tag)
            engine.memset(t[:].bitcast(I32), 0)
            return t

        xs = zeroed(nc.gpsimd, [P, WIDE], "xs")
        ws = zeroed(nc.vector, [P, E * PASSES * N], "ws")
        gs_low = zeroed(nc.vector, [P, T], "gs_low")
        gate_rows = tile([P, P], F32, "gate_rows")
        nc.gpsimd.memset(gate_rows[:], 0.0)
        ident = tile([P, P], F32, "ident")
        make_identity(nc, ident[:])
        adapter_scales = zeroed(nc.gpsimd, [P, H + N], "adapter_scales")
        was, wbs = adapter_scales[:, 0:H], adapter_scales[:, H:H + N]

        def load_expert_pair(h):
            words = tile([P, 2 * PASSES, 2 * N], U8, "ww%d" % h)
            nc.sync.dma_start(words[:].bitcast(I32), w_words[2 * h:2 * h + 2].rearrange("e s p b -> p (e s) b").bitcast(I32))
            return words

        def load_stacked_scales(plane, rows):
            for q in range(QUADS):
                nc.sync.dma_start(plane[32 * q:32 * q + 4 * rows.shape[0], :].bitcast(I32), rows[:, 4 * q:4 * q + 4, :].bitcast(I32))

        lst = sb.tile([P, T // 16], U16, name="lst")
        nc.sync.dma_start(lst[:], offs)
        load_stacked_scales(xs[:, 0:T], x_scales)
        xw = tile([P, PASSES, T], I32, "xw")
        nc.sync.dma_start(xw[:], x_words.rearrange("s p t d -> p s (t d)").bitcast(I32))
        lst2 = sb.tile([P, T // 16], U16, name="lst2")
        nc.sync.dma_start(lst2[:], offs2)
        ww = [load_expert_pair(0)]
        for q in range(QUADS):
            nc.sync.dma_start(
                ws[32 * q:32 * q + 4, :].bitcast(I32).rearrange("r (g n) -> r g n", g=E * PASSES),
                w_scales[:, :, 4 * q:4 * q + 4, :].rearrange("e s r n -> r (e s) n").bitcast(I32))
        for i, row in enumerate((gate, gate2)):
            nc.sync.dma_start(gate_rows[i * TILES:(i + 1) * TILES, :], row[0:1, :].rearrange("a (j m) -> (a j) m", m=P))
        ww.append(load_expert_pair(1))
        load_stacked_scales(was, wa_scales.rearrange("f s b n -> (f s) b n"))
        waw = tile([P, F * PASSES, H], I32, "waw")
        nc.sync.dma_start(waw[:], wa_words.rearrange("f s p i d -> p (f s) (i d)").bitcast(I32))
        load_stacked_scales(wbs, wb_scales.rearrange("f s b n -> (f s) b n"))
        wbw = tile([P, F, N], I32, "wbw")
        nc.sync.dma_start(wbw[:], wb_words.rearrange("f s p n d -> p (f s) (n d)").bitcast(I32))

        def gather_scales(offsets, name):
            scales = tile([P, T], U8, name)
            nc.vector.tensor_copy(scales[:], xs[:].indirect(offsets[:]))
            return scales

        def gather_words(offsets, h, name):
            words = []
            for s in range(PASSES):
                words.append(tile([P, HALF], U32, "%s%d%d" % (name, h, s)))
                nc.vector.tensor_copy(words[s][:], xw[:, s, :].bitcast(U32).indirect(entries(offsets, h * HALF, HALF)))
            return words

        gs = gather_scales(lst, "gs")
        nc.scalar.dma_start(gs_low[0:SHIFT_ROWS, :].bitcast(I32), gs[4:4 + SHIFT_ROWS, :].bitcast(I32))
        gw = [gather_words(lst, 0, "gw")]
        gs2 = gather_scales(lst2, "gs2")
        gw.append(gather_words(lst, 1, "gw"))
        gw2 = [gather_words(lst2, h, "gw2") for h in range(2)]


        def token_words(words, j, s):
            return words[j // 2][s][:, (j % 2) * P:(j % 2 + 1) * P].bitcast(FP8X4)

        gates_turned = bank(6, [P, P], "gates_turned")
        nc.tensor.transpose(gates_turned[:], gate_rows[:], ident[:])
        gate_cols = tile([P, 2 * TILES], F32, "gate_cols")
        nc.scalar.activation(gate_cols[:], gates_turned[:, 0:2 * TILES], COPY)

        def gated_rows(acc, col, first, count, name):
            rows = tile([P, count, P], F32, name)
            nc.scalar.activation(rows[:], acc[:].rearrange("s (m d) -> s d m", d=PACK)[:, first:first + count, :], COPY,
                                 scale=gate_cols[:, col:col + 1])
            return rows

        y_front = tile([P, 2, T], F32, "y_front")
        y_acc = [bank(e, [P, N], "y_acc%d" % e) for e in range(E)]
        for h in range(2):
            for s in range(PASSES):
                for e in (2 * h, 2 * h + 1):
                    g = e * PASSES + s
                    nc.tensor.matmul_mx(y_acc[e][:], lhsT=token_words(gw, e, s), lhsT_scale=(gs, gs_low)[s][:, e * P:(e + 1) * P],
                                        rhs=ww[h][:, g % (2 * PASSES), :].bitcast(FP4X4), rhs_scale=ws[:, g * N:(g + 1) * N],
                                        start=s == 0, stop=s == PASSES - 1)
            for e in (2 * h, 2 * h + 1):
                rows = gated_rows(y_acc[e], e, 0, 2, "y_rows_front%d" % e)
                turned = bank(4 + e % 2, [P, 2, P], "y_turned%d" % e)
                for d in range(2):
                    nc.tensor.transpose(turned[:, d, :], rows[:, d, :], ident[:])
                nc.scalar.copy(y_front[:, :, e * P:(e + 1) * P], turned[:])

        o_win = [tile([P, T if d < 2 else WIDE], F32, "o_win%d" % d) for d in range(PACK)]
        for first, count in ((0, P), (P, P), (2 * P, 2 * P)):
            for d in range(2):
                nc.vector.tensor_copy(o_win[d][:].indirect(entries(lst, first, count)), y_front[:, d, first:first + count])

        y_rows = [gated_rows(y_acc[e], e, 2, 2, "y_rows_back%d" % e) for e in range(E)]

        hb = tile([P, TILES, P, 2], F32, "hb")
        for f in range(F):
            h_turned = bank(6 + f, [P, 2, 2, P], "h_turned%d" % f)
            for jj in range(2):
                j = 2 * f + jj
                acc = bank(j, [P, H], "h_acc%d" % j)
                for s in range(PASSES):
                    nc.tensor.matmul_mx(acc[:], lhsT=token_words(gw2, j, s), lhsT_scale=gs2[4 * s:P, j * P:(j + 1) * P],
                                        rhs=waw[:, f * PASSES + s, :].bitcast(FP8X4), rhs_scale=was[4 * (f * PASSES + s):P, :],
                                        start=s == 0, stop=s == PASSES - 1)
                h_rows = tile([P, 2, P, 2], BF16, "h_rows%d" % j)
                nc.scalar.activation(h_rows[:], acc[:].rearrange("s (p u e) -> s u p e", u=2, e=2), RELU)
                pairs = h_rows[:].rearrange("s u p e -> s (u p e)").bitcast(F32)
                for u in range(2):
                    nc.tensor.transpose(h_turned[:, jj, u, :], pairs[:, u * P:(u + 1) * P], ident[:])
            nc.scalar.copy(hb[:, 2 * f:2 * f + 2, :, :], h_turned[:].rearrange("p j u s -> p j s u"))
        hq = tile([P, T], U32, "hq")
        hs = tile([P, T], U8, "hs")
        nc.vector.quantize_mx(hq[:].bitcast(FP8X4), hs[:], hb[:].rearrange("p j s u -> p (j s u)").bitcast(BF16))

        def slot_columns(rows, d, b, name):
            turned = bank(b, [P, T], name + "_turned")
            for j in range(TILES):
                nc.tensor.transpose(turned[:, j * P:(j + 1) * P], rows[j][:, d, :], ident[:])
            cols = tile([P, T], F32, name)
            nc.scalar.copy(cols[:], turned[:])
            return cols

        for d in range(2, PACK):
            cols = slot_columns(y_rows, d - 2, 7, "y_cols%d" % d)
            nc.vector.tensor_copy(o_win[d][:].indirect(lst[:]), cols[:])

        z_rows = []
        for j in range(TILES):
            f = j // 2
            acc = bank(j, [P, N], "z_acc%d" % j)
            nc.tensor.matmul_mx(acc[:], lhsT=hq[:, j * P:(j + 1) * P].bitcast(FP8X4), lhsT_scale=hs[:, j * P:(j + 1) * P],
                                rhs=wbw[:, f, :].bitcast(FP8X4), rhs_scale=wbs[4 * f:P, :], start=True, stop=True)
            z_rows.append(gated_rows(acc, TILES + j, 0, PACK, "z_rows%d" % j))

        total = tile([P, PACK, T], F32, "total")
        out_rows = out_0.rearrange("(p d) t -> p d t", d=PACK)
        z_win = []
        for d in range(PACK):
            cols = slot_columns(z_rows, d, 4 + d, "z_cols%d" % d)
            z_win.append(tile([P, WIDE], F32, "z_win%d" % d))
            nc.vector.tensor_copy(z_win[d][:].indirect(lst2[:]), cols[:])

        for d in range(PACK - 1):
            by_token = []
            for h in range(2):
                summed = bank(h, [P, HALF], "summed%d%d" % (d, h))
                for jj in range(2):
                    j = 2 * h + jj
                    for i, win in enumerate((o_win[d], z_win[d])):
                        nc.tensor.matmul(summed[:, jj * P:(jj + 1) * P], lhsT=win[:, j * P:(j + 1) * P], rhs=ident[:],
                                         is_transpose=True, start=i == 0, stop=i == 1)
                by_token.append(tile([P, HALF], F32, "by_token%d%d" % (d, h)))
                nc.scalar.copy(by_token[h][:], summed[:])
            for h in range(2):
                back = bank(2 + h, [P, HALF], "back%d%d" % (d, h))
                for jj in range(2):
                    nc.tensor.transpose(back[:, jj * P:(jj + 1) * P], by_token[h][:, jj * P:(jj + 1) * P], ident[:])
                nc.scalar.copy(total[:, d, h * HALF:(h + 1) * HALF], back[:])
            nc.sync.dma_start(out_rows[:, d, :], total[:, d, :])

        last = PACK - 1
        for h in (1, 0):
            cols = slice(h * HALF, (h + 1) * HALF)
            nc.vector.tensor_tensor(total[:, last, cols], o_win[last][:, cols], z_win[last][:, cols], ADD)
        nc.sync.dma_start(out_rows[:, last, :], total[:, last, :])

        grouped = tile([P, T, PACK], BF16, "grouped")

        def regroup(engine_copy, first, count):
            engine_copy(grouped[:, first:first + count, :].rearrange("p (c i) d -> p c d i", i=2),
                        total[:, :, first:first + count].rearrange("p d (c i) -> p c d i", i=2))

        regroup(nc.scalar.copy, 3 * P, P)
        regroup(nc.vector.tensor_copy, 2 * P, P)
        regroup(nc.vector.tensor_copy, 0, HALF)
        out_scales = tile([P, T], U8, "out_scales")
        words_out = out_1.rearrange("s p t d -> p (s t d)").bitcast(I32)
        for h in (1, 0):
            cols = slice(h * HALF, (h + 1) * HALF)
            codes = tile([P, HALF], U32, "codes%d" % h)
            nc.vector.quantize_mx(codes[:].bitcast(FP8X4), out_scales[:, cols], grouped[:, cols, :].rearrange("p t d -> p (t d)"))
            nc.sync.dma_start(words_out[:, cols], codes[:].bitcast(I32))
        for q in range(QUADS):
            queue = (nc.scalar, nc.sync)[q % 2]
            queue.dma_start(out_2[0, 4 * q:4 * q + 4, :].bitcast(I32), out_scales[32 * q:32 * q + 4, :].bitcast(I32))
